import numpy as np, ml_dtypes
CORES = [2,3,42,43,82,83,122,123]
N = 8
BF = ml_dtypes.bfloat16
R, D, CAP, MEETS = 64, 3, 256, (4, 3)
L = R * 4 ** D; P = (4 * L - R) // 3; I = P - L
OFF = [(R * 4 ** t - R) // 3 for t in range(D + 2)]
NODE = np.arange(P)
def rebuild(v):
    for t in range(D - 1, -1, -1):
        k = v[..., OFF[t + 1]:OFF[t + 2]]
        v[..., OFF[t]:OFF[t + 1]] = (k[..., 0::4] + 3 * k[..., 1::4] + 5 * k[..., 2::4] + 7 * k[..., 3::4]) & 255
    return v
def places(kids):
    c = kids.reshape(N, 8, 4, P); pl = np.zeros((N, 8, P), np.int64); pl[..., :R] = np.arange(R)
    for t in range(D):
        k = np.take_along_axis(c, pl[:, :, None, OFF[t]:OFF[t + 1]], 3)
        pl[..., OFF[t + 1]:OFF[t + 2]] = k.transpose(0, 1, 3, 2).reshape(N, 8, -1)
    return pl
def logical(dg, pl):
    return np.take_along_axis(dg.astype(np.float32).astype(np.int32).reshape(N, 8, 16, P), pl[:, :, None], 3)
def opened(v, m):
    o = np.any(v != v[np.arange(N) ^ m], axis=2)
    for t in range(D):
        o[..., OFF[t + 1]:OFF[t + 2]] &= np.repeat(o[..., OFF[t]:OFF[t + 1]], 4, axis=-1)
    return o
def meet(v, m):
    o = opened(v, m); u = v[np.arange(N) ^ m]; w = v.copy()
    up = o[..., I:] & (u[:, :, 15, I:] > v[:, :, 15, I:])
    w[..., I:] = np.where(up[:, :, None], u[..., I:], v[..., I:])
    return rebuild(w)
def put(rng, v):
    pl = np.concatenate([np.broadcast_to(np.arange(R), (N, 8, R)), R + np.argsort(rng.random((N, 8, P - R)), axis=-1)], axis=-1)
    k = np.zeros((N, 8, 4, P), np.int32); np.put_along_axis(k, pl[:, :, None, :I], pl[..., R:].reshape(N, 8, I, 4).transpose(0, 1, 3, 2).astype(np.int32), 3)
    e = np.zeros((N, 8, 16, P), np.float32); np.put_along_axis(e, pl[:, :, None], v.astype(np.float32), 3)
    return {"dg": e.reshape(N, 128, P).astype(BF), "kids": k.reshape(N, 32, P)}
def whole(rng, *shape):
    return rng.integers(0, 256, shape, dtype=np.int32)
def pool(rng):
    par = np.argsort(rng.random((8, L // 4)), axis=1)[:, :CAP // 8]; m = np.zeros((8, L // 4, 4), bool); np.put_along_axis(m, par[:, :, None], True, 1)
    m = m.reshape(8, L); np.put_along_axis(m, np.argsort(rng.random((8, L)), axis=1)[:, :CAP // 2 - 2], True, 1); m[:, 0] = True; m[:, -1] = True
    return m, par
def change(rng, base, m, x):
    mod = m & (rng.random((N, 8, L)) < 0.6); one = rng.random((N, 8, 1, L)) < 0.3
    c = mod[:, :, None] & (~one | (np.arange(16)[:, None] == rng.integers(0, 16, (N, 8, 1, L))))
    c[:, :, 15] &= rng.random((N, 8, L)) >= 0.25
    return np.ascontiguousarray(np.where(c, x, base))
def collide(rng, base, x, par):
    k = np.take_along_axis(base.reshape(8, 16, L // 4, 4), par[:, None, :, None], 2); k = np.repeat(k[None], N, axis=0)
    e = rng.integers(1, 256, k.shape[:-1], dtype=np.int32); k[..., 0] = (k[..., 0] - 3 * e) & 255; k[..., 1] = (k[..., 1] + e) & 255
    w = x.reshape(N, 8, 16, L // 4, 4).copy(); np.put_along_axis(w, par[None, :, None, :, None], k, 3); return w.reshape(N, 8, 16, L)
def grow(rng, base, x, m, hide, own):
    v = np.zeros((N, 8, 16, P), np.int32); v[..., I:] = x; rebuild(v); b = np.zeros((8, 16, P), np.int32); b[..., I:] = base; rebuild(b)
    cl = np.zeros((8, P), bool); cl[:, I:] = m
    for t in range(D - 1, -1, -1):
        cl[:, OFF[t]:OFF[t + 1]] = np.any(cl[:, OFF[t + 1]:OFF[t + 2]].reshape(8, -1, 4), axis=2)
    h = cl & (rng.random((8, P)) < hide) & (NODE < I); v = np.where(h[:, None], b, v)
    o = cl & (rng.random((N, 8, P)) < own) & (NODE < I); v = np.where(o[:, :, None], whole(rng, N, 8, 16, P), v)
    s = ~cl & (rng.random((8, P)) < 0.02) & (NODE < I)
    return np.where(s[:, None], whole(rng, 8, 16, P), v)
def balance(rng, v, m):
    a = np.arange(16)[:, None]; low = (np.arange(N) < (np.arange(N) ^ MEETS[0]))[:, None, None, None]
    for t in range(D):
        n = R * 4 ** t; k = np.any(m.reshape(8, n, -1), axis=2)
        e = rng.integers(1, 32, (N, 8, 1, n)) * rng.choice(np.array([-1, 1]), (N, 8, 1, n))
        if t % 2 == 0:
            s = rng.integers(0, 16, (N, 8, 1, n)); c = 1 * (a == s) - 1 * (a == ((s + rng.integers(1, 16, (N, 8, 1, n))) & 15))
        else:
            s = rng.integers(0, 14, (N, 8, 1, n)); c = 1 * (a == s) - 2 * (a == s + 1) + 1 * (a == s + 2)
        z = rng.integers(64, 192, (8, 16, n)) + low * e * c
        v[..., OFF[t]:OFF[t + 1]] = np.where(k[:, None], z, v[..., OFF[t]:OFF[t + 1]])
    return v
def setup_inputs(rng):
    base = whole(rng, 8, 16, L); m, par = pool(rng); x = change(rng, base, m, whole(rng, N, 8, 16, L)); x = collide(rng, base, x, par[:, :CAP // 32])
    return put(rng, grow(rng, base, x, m, 0.1 * (NODE >= OFF[D - 1]), 0.05))
def setup_inputs_full(rng):
    base = whole(rng, 8, 16, L); m = np.zeros((8, L), bool); t = [t for t in range(D + 1) if R * 4 ** t >= CAP][0]; w = 4 ** (D - t)
    for i, g in enumerate(rng.permutation(8)):
        if i % 4 == 1: l = (4 * rng.permutation(L // 4)[:CAP // 4, None] + np.arange(4)).reshape(-1)
        elif i % 4 == 3: l = np.arange(L - CAP, L)
        else: l = rng.permutation(R * 4 ** t)[:CAP] * w + rng.integers(0, w, CAP)
        m[g, l] = True
    z = whole(rng, N, 8, 16, L)
    for s in (0, 15): z[:, :, s] = (z[0, :, s].copy() + 31 * np.arange(N)[:, None, None]) & 255
    v = grow(rng, base, np.where(m[:, None], z, base), m, 0.0, 0.0)
    return put(rng, balance(rng, v, m & (rng.random((8, L)) < 0.5)))
def setup_inputs_ties(rng):
    base = whole(rng, 8, 16, L); base[:, 15] = rng.choice(np.array([0, 1, 254, 255]), (8, L)); m, par = pool(rng)
    x = change(rng, base, m, whole(rng, N, 8, 16, L)); c = np.any(x != base, axis=2)
    x[:, :, 15] = np.where(c, np.clip(base[:, 15] + rng.choice(np.array([-1, 0, 0, 1]), (N, 8, L)), 0, 255), base[:, 15])
    return put(rng, grow(rng, base, x, m, 0.0, 0.05))
def setup_inputs_hidden(rng):
    base = whole(rng, 8, 16, L); m, par = pool(rng); x = change(rng, base, m, whole(rng, N, 8, 16, L)); x = collide(rng, base, x, par)
    return put(rng, grow(rng, base, x, m, 0.15, 0.3))
def setup_inputs_calm(rng):
    base = whole(rng, 8, 16, L); m, par = pool(rng); p = rng.permutation(8); a = int(rng.integers(0, N)); m[p[:5]] = False; m[p[3], 0] = True; m[p[4], -1] = True
    x = change(rng, base, m, whole(rng, N, 8, 16, L))
    for g, l in ((p[3], 0), (p[4], L - 1)):
        x[:, g, :, l] = base[g, :, l]; x[a ^ MEETS[1], g, :, l] = (base[g, :, l] + rng.integers(1, 256, 16)) & 255
    v = grow(rng, base, x, m, 0.0, 0.0); v[a ^ MEETS[0]] = v[a]; return put(rng, v)
def setup_inputs_spread(rng):
    def uneven(*shape):
        u = rng.random(shape, dtype=np.float32); u = u * u * u; u = np.minimum(256 * u * u, 255).astype(np.int32)
        return np.where(rng.random(shape, dtype=np.float32) < 0.1, np.int32(255), u)
    base = uneven(8, 16, L) * (rng.random((8, 1, L)) > 0.0625).astype(np.int32); m, par = pool(rng)
    x = change(rng, base, m, uneven(N, 8, 16, L)); x = collide(rng, base, x, par[:, :CAP // 32])
    return put(rng, grow(rng, base, x, m, 0.1 * (NODE >= OFF[D - 1]), 0.05))
def check_inputs(d):
    bad = []; v = d["dg"].astype(np.float32); k = d["kids"].astype(np.int64)
    if not (np.isfinite(v).all() and (v == np.floor(v)).all() and v.min() >= 0 and v.max() <= 255): bad.append("symbols")
    if k.min() < 0 or k.max() >= P: return bad + ["children"]
    pl = places(k)
    if (np.sort(pl, axis=-1) != NODE).any(): bad.append("places")
    elif np.take_along_axis(k.reshape(N, 8, 4, P), pl[:, :, None, I:], 3).any(): bad.append("leaves")
    if bad: return bad
    v = logical(d["dg"], pl)
    for m in MEETS:
        o = opened(v, m)
        if max(int(np.count_nonzero(o[..., OFF[t]:OFF[t + 1]], axis=-1).max()) for t in range(D + 1)) > CAP: return ["open nodes"]
        v = meet(v, m)
    return []
def reference(dg, kids):
    pl = places(kids); v = logical(dg, pl)
    for m in MEETS:
        v = meet(v, m)
    y = np.zeros((N, 8, 16, P), np.float32); np.put_along_axis(y, pl[:, :, None], v.astype(np.float32), 3)
    return {"y": y.reshape(N, 128, P).astype(BF)}

from concourse.bass import DstId, RemoteDMATransfer
from concourse.mybir import AluOpType as Op, ActivationFunctionType as Act

P, L, PAD, Q = 5440, 4096, 256, 1360
MEETS = (4, 3)
SCRATCH = {}
for _t, _d in (
    ("bfloat16", dict(Y=PAD + P, LF=PAD + L + 16, I2=PAD + 1040, S2=1024, S01=320, I01=320, XP=144, D=144, IOS=256, W=16,
                      SQ=432, RF=144, RC=144, RV=144, RQ=144, RN=144, RU=144, PK=144, EM=144, B=128, TL=128, TG=128,
                      BD=128, ID=13 * 128, WU=128, QA=128, QB=128, QC=128, TMP=128, TMP2=128, C2K=256, M1=256, M2=1024,
                      qb=80, YB=1024, N2=512, N01=320, O0=256, VD=256, GT=256, SG=256, t1=256, t2=256, F=256, R=288,
                      T2=16, T3=256, C1=256, C2=256, C3=256, ab=16, bb=16, OH=256, OU=256, KEEP=272, VF=256,
                      V0=256, V1=256, out0=256, out1=256, lv0=256, lv1=256, ll0=256, ll1=256, li0=320, li1=320)),
    ("float32", dict(XF=8, CF=16, SW0=16, SW=16, SWa=16, SWb=16, RG=144, A=144, Q4=128, G0=64, G1=256, G2=1024, qt=80,
                     qo=80, TAB3=256, TAB2=256, CV=512, QS=256, OLD=256, tm=256, SA=256, Z=512, a1=16, a3=16, a4=16,
                     a5=16, a6=16)),
    ("int32", dict(Kq=Q, K0=64, PI=1, XI=8, NI=576, NV=576)),
    ("uint16", dict(ql=80, ol=80, IL=80, L3=256, LS=36, LS2=64, al=16, bl=16, xl=16, q2=16, l2=16, lY=16, lF=16,
                    pk0=512, pk1=512, lp0=512, lp1=512)),
):
    for _n in _d:
        SCRATCH[_n] = ("sbuf", [128, _d[_n]], _t)
for _b in range(8):
    SCRATCH["p%d" % _b] = ("psum", [128, 512], "float32")

MSG = {
    "ra": (0, "S01", "li0", 0, 32, True),
    "rb": (0, "S01", "li0", 32, 64, False),
    "l1": (0, "S01", "li0", 64, 320, False),
    "pa0": (0, "pk0", "lp0", 0, 256, True),
    "pb0": (0, "pk0", "lp0", 256, 512, False),
    "va": (0, "V0", "lv0", 0, 128, False),
    "vb": (0, "V0", "lv0", 128, 256, False),
    "lf0": (0, "out0", "ll0", 0, 256, False),
    "v1": (1, "V1", "lv1", 0, 256, True),
    "pa1": (1, "pk1", "lp1", 0, 256, True),
    "pb1": (1, "pk1", "lp1", 256, 512, False),
    "i01": (1, "I01", "li1", 0, 320, False),
    "lf1": (1, "out1", "ll1", 0, 256, False),
}
HELPED = [k for k in MSG if MSG[k][5]]
SEMAPHORES = ["m_" + k for k in MSG] + ["sent"] + ["d%d" % i for i in range(7)] + ["c%d" % i for i in range(120)]


def helper_of(rank, T, topo):
    core = T.cores[rank]
    here = [c for c in T.cores if topo.chip(c) == topo.chip(core)]
    free = [c for c in topo.cores_of(core) if topo.die(c) != topo.die(core) and T.rank_of(c) is None
            and all(topo.may_write(c, T.cores[rank ^ m]) for m in MEETS)]
    return free[here.index(core)]


def home_mask(rank, T, topo):
    core = T.cores[rank]
    return topo.mask(core, helper_of(rank, T, topo)) & ~topo.mask(core, T.cores[rank ^ MEETS[0]])


def bits(mask):
    return bin(mask).count("1")


def A_(name, a=0, b=None, s=1):
    return (name, a, SCRATCH[name][1][1] if b is None else b, s)


def col(name, j):
    return (name, j, j + 1, 1)


def hf(name, h):
    return (name, 128 * h, 128 * h + 128, 1)


def ind(win, off):
    return ("*", A_(win) if isinstance(win, str) else win, A_(off) if isinstance(off, str) else off)


def rank_program(g, core, T, topo):
    rank = T.rank_of(core)

    def ap(x):
        if x[0] == "*":
            return ap(x[1]).indirect(ap(x[2]))
        return T[x[0]][:, x[1]:x[2]:x[3]] if x[3] != 1 else T[x[0]][:, x[1]:x[2]]

    def write(items):
        args = []
        for src, key, dst, mask in items:
            rid, pid, _ = topo.addr(dst)
            a, b = MSG[key][3:5]
            args.append((ap(A_(MSG[key][2], a, b)), ap(A_(src, a, b)), T.sem["m_" + key], pid, rid, mask))
        if len(args) == 1:
            o, i, s, pid, rid, mask = args[0]
            g.remote_dma(o, i, s, T.sem.sent, pid, rid, mask)
        else:
            g.remote_dma_fused([RemoteDMATransfer(dst_ids=[DstId(rid=rid, pnc=pid)], dma_engine_mask=mask, remote_sem=s, src=i, dst=o)
                                for o, i, s, pid, rid, mask in args], local_sem=T.sem.sent)
        return sum(bits(x[5]) for x in args)

    if rank is None:
        owner = [r for r in range(len(T.cores)) if helper_of(r, T, topo) == core]
        if not owner:
            return
        total = 0
        for key in HELPED:
            dst = T.cores[owner[0] ^ MEETS[MSG[key][0]]]
            g.wait_ge(T.sem["m_" + key], bits(home_mask(owner[0], T, topo)))
            total += write([(MSG[key][2], key, dst, topo.mask(core, dst))])
        g.wait_ge(T.sem.sent, total)
        return

    helper = helper_of(rank, T, topo)
    ops = []

    def rec(q, fns, reads, writes, acc=False, kind="c", token=None):
        rd, wr = [], []
        for x in reads:
            if isinstance(x, tuple):
                rd += [x[1], x[2]] if x[0] == "*" else [x]
        for x in writes:
            if x[0] == "*":
                wr.append(x[1])
                rd.append(x[2])
            else:
                wr.append(x)
        ops.append({"q": q, "fns": fns, "rd": rd, "wr": wr, "acc": acc, "kind": kind, "token": token})

    def nm(*xs):
        return [A_(x) if isinstance(x, str) else x for x in xs]

    def sc(x):
        return ap(x) if isinstance(x, tuple) else x

    def ts(out, in0, s1, op0, s2=None, op1=None):
        out, in0 = nm(out, in0)
        if op1 is None:
            rec("v", [lambda: g.vector.tensor_scalar(ap(out), ap(in0), sc(s1), None, op0)], [in0, s1], [out])
        else:
            rec("v", [lambda: g.vector.tensor_scalar(ap(out), ap(in0), sc(s1), sc(s2), op0, op1)], [in0, s1, s2], [out])

    def tt(out, a, b, op):
        out, a, b = nm(out, a, b)
        rec("v", [lambda: g.vector.tensor_tensor(ap(out), ap(a), ap(b), op)], [a, b], [out])

    def cp(out, a):
        out, a = nm(out, a)
        rec("v", [lambda: g.vector.tensor_copy(ap(out), ap(a))], [a], [out])

    def ms(out, c):
        out, = nm(out)
        rec("v", [lambda: g.vector.memset(ap(out), c)], [], [out])

    def scan(out, d0, d1, op0, op1):
        out, d0, d1 = nm(out, d0, d1)
        rec("v", [lambda: g.vector.tensor_tensor_scan(ap(out), ap(d0), ap(d1), 0.0, op0, op1)], [d0, d1], [out])

    def act(out, a, func=Act.Copy, **kw):
        out, a = nm(out, a)
        rec("s", [lambda: g.scalar.activation(ap(out), ap(a), func, **{k: sc(kw[k]) for k in kw})], [a, kw.get("bias")], [out])

    def mm(out, pairs):
        pairs = [nm(*pr) for pr in pairs]
        n = len(pairs)
        fns = [(lambda i=i: g.tensor.matmul(ap(out), ap(pairs[i][0]), ap(pairs[i][1]), i == 0, i == n - 1)) for i in range(n)]
        rec("t", fns, [x for pr in pairs for x in pr], [out], acc=True)

    def mms(trip):
        fns = [(lambda t=t: g.tensor.matmul(ap(t[0]), ap(t[1]), ap(t[2]), True, True)) for t in trip]
        rec("t", fns, [x for t in trip for x in t[1:]], [t[0] for t in trip])

    def iota(out, pattern, cm, **kw):
        rec("g", [lambda: g.iota(ap(A_(out)), pattern, 0, cm, **kw)], [], [A_(out)])

    def load(q, out, src, after=()):
        eng = g.sync if q == "y" else g.scalar
        rec(q, [lambda: eng.dma_start(ap(out), src)], list(after), [out], kind="d")

    sent = [0]

    def send(*keys):
        items = []
        for key in keys:
            other = T.cores[rank ^ MEETS[MSG[key][0]]]
            items.append((MSG[key][1], key) + ((helper, home_mask(rank, T, topo)) if MSG[key][5] else (other, topo.mask(core, other))))

        def fn():
            sent[0] += write(items)
        rec("g", [fn], [A_(MSG[k][1], MSG[k][3], MSG[k][4]) for k in keys], [], kind="r")

    for key in MSG:
        other = rank ^ MEETS[MSG[key][0]]
        src = helper_of(other, T, topo) if MSG[key][5] else T.cores[other]
        rec(None, [], [], [A_(MSG[key][2], MSG[key][3], MSG[key][4])], kind="x", token=("m_" + key, len(topo.engines(src, core))))

    def wrap(master, src, a=0, b=256):
        return [(A_(master, 15 - i, 143 - i), A_(src, a + i, b, 16)) for i in range(16)]

    def ps(bank, a=0, b=256):
        return A_("p%d" % bank, a, b)

    def route(out, src, a, b):
        mm(out, [(A_("A", 12 - 4 * j, 140 - 4 * j), A_(src, a + j, b, 4)) for j in range(4)])

    def split(src, a, b):
        ts(A_("qb", a, b), src, 1.0 / Q, Op.mult, 130.0 - 0.5 * (Q - 1) / Q, Op.add)
        ts(A_("ql", a, b), A_("qb", a, b), -130.0, Op.add)
        ts(A_("qt", a, b), A_("qb", a, b), -float(Q), Op.mult, 130.0 * Q, Op.add)
        tt(A_("qo", a, b), A_("qt", a, b), src, Op.add)
        cp(A_("ol", a, b), A_("qo", a, b))

    load("s", A_("S01", 0, 64), T.dg[:, 0:64])
    load("y", A_("K0"), T.kids[:, 0:256])
    load("y", A_("Kq"), T.kids[:])
    load("y", A_("Y", PAD, PAD + P // 2), T.dg[:, 0:P // 2])
    load("y", A_("Y", PAD + P // 2, PAD + P), T.dg[:, P // 2:P], after=[A_("Kq")])
    iota("PI", [[0, 1]], 1)
    iota("XP", [[1, 144]], -1, allow_small_or_imprecise_dtypes=True)
    iota("IOS", [[1, 256]], 0, allow_small_or_imprecise_dtypes=True)
    iota("SW0", [[16, 16]], 0, allow_small_or_imprecise_dtypes=True)
    send("ra")
    send("rb")
    SH, AND = Op.logical_shift_right, Op.bitwise_and
    ts(col("XI", 0), "PI", 15, AND)
    ts(col("XI", 1), "PI", 2, SH, 3, AND)
    ts(col("XI", 2), "PI", 3, AND)
    ts(col("XI", 3), "PI", 1, SH, 7, AND)
    ts(col("XI", 4), "PI", 1, AND)
    ts(col("XI", 5), "PI", 3, SH, 1, AND)
    ms(A_("LF", PAD + L), 0.0)
    ms(A_("I2", PAD + 1024), 0.0)
    ms("KEEP", 0.0)
    ms(A_("R", 0, 16), 0.0)
    ms("C2K", 2064.0)
    cp(A_("XF", 0, 6), A_("XI", 0, 6))
    cm, ck, cq, cm2, cpar, ch = [col("XF", j) for j in range(6)]
    cPK, sPK, lt15, eq15, eq0, bE, bQ, m1, wq, lt64, lt4, q3, n15 = [col("CF", j) for j in range(13)]
    Dn = A_("D", 0, 128)
    ts("D", "XP", cm, Op.add)
    ts("W", A_("IOS", 0, 16), cq, Op.is_equal)
    ts(bE, ch, -4.0, Op.mult, -9.5, Op.add)
    ts(bQ, ck, -4.0, Op.mult, -1.5, Op.add)
    ts("A", "D", ck, Op.subtract, 12.0, Op.is_equal)
    ts(A_("ID", 0, 128), Dn, cm, Op.is_equal)
    ts("G0", "K0", col("W", 0), Op.mult)
    route(ps(0, 0, 16), "G0", 0, 64)
    ts(cPK, cm2, 8.0, Op.add)
    ts(sPK, cpar, 255.0, Op.mult, 1.0, Op.add)
    ts(lt15, cm, 15.0, Op.is_lt)
    ts(eq15, cm, 15.0, Op.is_equal)
    ts(eq0, cm, 0.0, Op.is_equal)
    ts(m1, cm, 1.0, Op.add)
    ts(wq, cq, 2.0, Op.mult, 1.0, Op.add)
    ts(lt64, cm, 15.0, Op.is_lt, 64.0, Op.mult)
    ts(lt4, cm, 15.0, Op.is_lt, 4.0, Op.mult)
    act(A_("SQ", 0, 128), Dn, Act.Square, bias=-7.5)
    act(A_("SQ", 144, 288), "D", Act.Square, bias=bE)
    act(A_("SQ", 288, 416), Dn, Act.Square, bias=bQ)
    scales = [1, 3, 5, 7, 9, 15, 21, 25, 35, 49, 16, 4, -1]
    ident = {w: A_("ID", 128 * j, 128 * j + 128) for j, w in enumerate(scales)}
    for w in scales[1:7]:
        act(ident[w], ident[1], Act.Copy, scale=float(w))
    split(ps(0, 0, 16), 0, 16)
    act("M1", ind("W", A_("ql", 0, 16)))
    for w in scales[7:]:
        act(ident[w], ident[1], Act.Copy, scale=float(w))
    cp(A_("IL", 0, 16), ps(0, 0, 16))
    ts(A_("LS", 20, 36), ps(0, 0, 16), float(PAD), Op.add)
    ts(q3, cq, 3.0, Op.is_equal)
    ts(n15, cm, 15.0, Op.is_equal, -4096.0, Op.mult)
    ts("SW", "SW0", cm, Op.add)
    ts("SWa", "SW0", cm, Op.add, -float(PAD), Op.add)
    ts("SWb", "SW0", cm, Op.add, 8192.0 - PAD, Op.add)
    ts("PK", "D", cPK, Op.is_equal, sPK, Op.mult)
    ts("RV", "D", 15.0, Op.is_equal, eq15, Op.mult)
    tt("G1", ind("Kq", A_("ol", 0, 16)), "M1", Op.mult)
    route(ps(2, 0, 64), "G1", 0, 256)
    ts("RF", "D", 15.0, Op.is_equal)
    ts("RC", "D", 15.0, Op.is_equal, lt15, Op.mult)
    ts("RQ", "D", 15.0, Op.is_equal, q3, Op.mult)
    ts("RN", "D", 15.0, Op.is_equal, n15, Op.mult)
    ts("RU", "D", 15.0, Op.is_equal, 8192.0, Op.mult)
    ts("RG", "D", 15.0, Op.is_equal)
    ts("TMP", Dn, cm, Op.is_ge)
    ts("TMP2", Dn, m1, Op.is_equal, lt15, Op.mult)
    split(ps(2, 0, 64), 16, 80)
    for u in range(4):
        act(A_("M2", 256 * u, 256 * u + 256), ind("W", A_("ql", 16 + 16 * u, 32 + 16 * u)))
    cp(A_("IL", 16, 80), ps(2, 0, 64))
    ts("LS2", ps(2, 0, 64), float(PAD), Op.add)
    for u in range(4):
        tt(A_("G2", 256 * u, 256 * u + 256), ind("Kq", A_("ol", 16 + 16 * u, 32 + 16 * u)), A_("M2", 256 * u, 256 * u + 256), Op.mult)
        route(ps(5, 64 * u, 64 * u + 64), "G2", 256 * u, 256 * u + 256)
    ts("Q4", A_("SQ", 288, 416), 4.0, Op.is_lt)
    ts("B", A_("SQ", 0, 128), 64.0, Op.is_lt)
    ts("EM", A_("SQ", 144, 288), 4.0, Op.is_lt)
    ts(A_("LS", 16, 20), A_("SW", 0, 4), float(PAD), Op.add)
    tt("BD", "TMP2", ident[1], Op.subtract)
    tt("TL", "TMP", "B", Op.mult)
    ts("WU", "B", wq, Op.mult)
    ts("QA", "B", lt64, Op.mult)
    ts("QB", "B", lt4, Op.mult)
    ts("QC", "B", q3, Op.mult)
    tt("TG", "B", "TL", Op.subtract)
    mm(ps(6), [("Q4", "G1")])

    Yw = A_("Y", PAD)

    def pack(h, src, a):
        mm(ps(h), [(A_("PK", 8 - 8 * j, 136 - 8 * j), A_(src, a + 512 * h + j, a + 512 * h + 512, 2)) for j in range(2)])

    def pack_out(mt, h):
        cp(A_("pk%d" % mt, 256 * h, 256 * h + 256), ps(h))

    cp(A_("S2", 0, 512), ind(Yw, A_("IL", 16, 48)))
    cp("L3", ps(5))
    act(A_("S01", 64, 320), ind(Yw, A_("IL", 0, 16)))
    send("l1")
    act(A_("S2", 512, 1024), ind(Yw, A_("IL", 48, 80)))
    pack(0, "S2", 0)
    pack(1, "S2", 0)
    pack_out(0, 0)
    send("pa0")
    for u in range(4):
        a = PAD + 1024 * u
        cp(A_("LF", a, a + 512), ind(Yw, A_("L3", 64 * u, 64 * u + 32)))
        if u == 0:
            pack_out(0, 1)
            send("pb0")
        act(A_("LF", a + 512, a + 1024), ind(Yw, A_("L3", 64 * u + 32, 64 * u + 64)))
        if u == 2:
            act(hf("V0", 0), ps(2, 0, 128))
            send("va")
        mm(ps(2 + 5 * (u // 2), 64 * u, 64 * u + 64), wrap("RV", "LF", a, a + 1024))
    act(hf("V0", 1), ps(7, 128, 256))
    send("vb")
    act("TAB3", ps(5), Act.Identity, bias=float(PAD))
    act("TAB2", ps(6), Act.Identity, bias=float(PAD))

    def base(u):
        a, bank = PAD + 1024 * u, ps((3, 4, 2, 7)[u])
        mm(bank, [("B", "C2K")] + [(ident[2 * k + 1], A_("LF", a + k, a + 1024, 4)) for k in range(4)])
        act(A_("YB", 256 * u, 256 * u + 256), bank, Act.Identity, bias=-127.5)

    def sub(u):
        tt(A_("I2", PAD + 256 * u, PAD + 256 * u + 256), ps((3, 4, 2, 7)[u]), A_("YB", 256 * u, 256 * u + 256), Op.subtract)

    def put(lst, src, a, e):
        cp(ind("Y", A_(lst, 8 * e, 8 * e + 8)), A_(src, a + 128 * e, a + 128 * e + 128))

    def bo(e):
        put("LS2", "I2", PAD, e)

    c0, c1, c2 = ps(5), ps(5, 256, 512), (ps(6, 0, 128), ps(4, 0, 128))

    def cmp2(mt, h):
        cp(A_("CV", 256 * h, 256 * h + 256), A_("lp%d" % mt, 256 * h, 256 * h + 256))
        tt(A_("N2", 256 * h, 256 * h + 256), A_("CV", 256 * h, 256 * h + 256), ps(h), Op.not_equal)
        mm(c2[h], [(A_("EM", 8 - 8 * e, 136 - 8 * e), A_("N2", 256 * h + e, 256 * h + 256, 2)) for e in range(2)])

    def cmp01(mt):
        tt("N01", ("S01", "I01")[mt], "li%d" % mt, Op.not_equal)
        mms([(c1, A_("B"), A_("N01", 64, 320))] + [(A_("p5", k, 256, 4), A_("B"), A_("N01", 0, 64)) for k in range(4)])

    def signs(mt):
        bank = ps(7) if mt else ps(1, 256, 512)
        mm(bank, [(ident[1], "lv%d" % mt), (ident[-1], "V%d" % mt)])
        act("SG", bank, Act.Sign)
        if mt == 1:
            act("VD", "SG", Act.Abs)
        act("GT", "SG", Act.Relu)

    def compact(mt, fill):
        scan(A_("R", 16, 272), "F", "F", Op.add, Op.max)
        cp(A_("R", 272, 288), A_("R", 31, 272, 16))
        fill[0]()
        mm(ps(5, 0, 17), wrap("RF", "R", 16, 288))
        mm(ps(6), [("TL", A_("R", 16, 272)), ("TG", A_("R", 15, 271))])
        ts("C1", "IOS", col("p5", 16), Op.is_ge)
        fill[1]()
        act("T2", ps(5, 0, 16))
        act("T3", ps(6))
        mm(ps(0, 0, 16), wrap("RC", "C1"))
        cp("al", ps(0, 0, 16))
        act("ab", ps(0, 0, 16))
        tt("C2", ind("T2", "al"), "IOS", Op.is_le)
        fill[2]()
        mm(ps(1, 0, 16), [(ident[16], "ab")] + wrap("RC", "C2"))
        cp("bl", ps(1, 0, 16))
        act("bb", ps(1, 0, 16))
        tt("C3", ind("T3", "bl"), "IOS", Op.is_le)
        fill[3]()
        mm(ps(0, 16, 32), [(ident[16], "bb")] + wrap("RF", "C3"))
        cp("xl", ps(0, 16, 32))
        win, out = A_("LF", PAD), "out%d" % mt
        cp(hf(out, 0), ind(win, A_("xl", 0, 8)))
        act(hf(out, 1), ind(win, A_("xl", 8, 16)))
        send("lf%d" % mt)

    def places():
        tt(A_("Z", 0, 256), ind("TAB3", "bl"), "OU", Op.mult)
        tt(A_("Z", 256, 512), ind("TAB2", "bl"), "OH", Op.mult)
        mm(ps(4, 0, 32), wrap("RG", "Z", 0, 512))

    def prepare(mt):
        mm(ps(7), [("BD", "C3")])
        mm(ps(2), [("QA", "C1"), ("QB", "C2"), ("QC", "C3")])
        mm(ps(4, 0, 16), [(ident[4], "bb")] + wrap("RQ", "C3"))
        act("OH", ps(7), Act.Identity, bias=eq0)
        act("QS", ps(2))
        tt("OU", ind("GT", "bl"), "OH", Op.mult)
        cp("q2", ps(4, 0, 16))
        mm(ps(3), [("WU", "OU")])
        act("OLD", ind(A_("I2", PAD), "q2"), Act.Identity, bias=4096.0)
        tt(A_("KEEP", 1, 256), ps(2, 1, 256), A_("QS", 0, 255), Op.is_equal)
        mm(ps(5, 0, 16), [(ident[4], "bb")] + wrap("RQ", "C3") + wrap("RN", "KEEP", 1, 257))
        if mt == 0:
            mm(ps(6, 0, 16), [(ident[16], "bb")] + wrap("RF", "C3") + wrap("RU", "OU"))
        tt("tm", "out%d" % mt, ps(3), Op.mult)
        if mt == 0:
            tt("VF", "lv0", "F", Op.mult)
        else:
            places()
        scan(ps(7), A_("KEEP", 0, 256), "tm", Op.mult, Op.add)
        if mt == 0:
            tt("V1", "VF", "V0", Op.max)
            send("v1")
        tt("a4", ps(5, 0, 16), "SWa", Op.max)
        tt("SA", "OLD", ps(7), Op.subtract)
        ts("a1", ps(5, 0, 16), 0.0, Op.is_ge)
        ts("l2", "a4", float(PAD), Op.add)

    def place_lists():
        tt("a3", ps(4, 16, 32), "a1", Op.mult)
        tt("a5", ps(4, 0, 16), "SW", Op.max)
        tt("a6", "a3", "SW", Op.max)
        cp("lY", "a5")
        cp(A_("LS", 0, 16), "a6")

    def update(mt):
        tt("tm", "ll%d" % mt, ps(3), Op.mult)
        scan(ps(7), A_("KEEP", 0, 256), "tm", Op.mult, Op.add)
        tt(A_("NI", 0, 256), ps(7), "SA", Op.add)
        ts(A_("NV", 0, 256), A_("NI", 0, 256), 255, AND)
        cp(ind("I2", "l2"), A_("NV", 0, 256))

    def upper():
        mm(ps(6, 64, 320), [(ident[2 * k + 1], A_("I2", PAD + k, PAD + 1024, 4)) for k in range(4)])
        mm(ps(6, 0, 64), [(ident[(2 * (j // 4) + 1) * (2 * (j % 4) + 1)], A_("I2", PAD + j, PAD + 1024, 16)) for j in range(16)])

    def upper_mod():
        cp(A_("NI", 256, 576), ps(6, 0, 320))
        ts(A_("NV", 256, 576), A_("NI", 256, 576), 255, AND)

    base(0)
    base(1)
    sub(0)
    cmp01(0)
    act("O0", c0, Act.Sign)
    sub(1)
    cmp2(0, 1)
    base(2)
    base(3)
    tt("t1", "O0", c1, Op.min)
    bo(0)
    tt(hf("VD", 0), hf("lv0", 0), hf("V0", 0), Op.not_equal)
    tt(hf("t2", 1), hf("t1", 1), c2[1], Op.min)
    tt(hf("t2", 0), hf("t1", 0), hf("VD", 0), Op.min)
    cmp2(0, 0)
    tt(hf("VD", 1), hf("lv0", 1), hf("V0", 1), Op.not_equal)
    signs(0)
    tt(hf("F", 1), hf("t2", 1), hf("VD", 1), Op.min)
    tt(hf("F", 0), hf("t2", 0), c2[0], Op.min)
    compact(0, [lambda: [sub(2), sub(3)], lambda: bo(1), lambda: bo(2), lambda: bo(3)])
    prepare(0)
    bo(4)
    tt("a5", ps(6, 0, 16), "SWb", Op.max)
    bo(5)
    ts("lF", "a5", PAD - 8192.0, Op.add)
    update(0)
    pack(0, "I2", PAD)
    pack(1, "I2", PAD)
    upper()
    pack_out(1, 0)
    pack_out(1, 1)
    send("pa1", "pb1")
    places()
    upper_mod()
    cp("I01", A_("NV", 256, 576))
    send("i01")
    signs(1)
    cp(ind("LF", "lF"), "ll0")
    bo(6)
    place_lists()
    cmp2(1, 1)
    tt(hf("t1", 1), hf("VD", 1), c2[1], Op.min)
    cmp2(1, 0)
    cmp01(1)
    tt(hf("t1", 0), hf("VD", 0), c2[0], Op.min)
    tt("t2", "t1", c1, Op.min)
    tt("F", "t2", c0, Op.min)
    compact(1, [lambda: put("LS", "NV", 0, 0), lambda: put("LS", "NV", 0, 1), lambda: put("lY", "ll0", 0, 0), lambda: put("lY", "ll0", 0, 1)])
    prepare(1)
    bo(7)
    update(1)
    upper()
    place_lists()
    cp(ind("Y", "lY"), "ll1")
    upper_mod()
    cp(ind("Y", "LS"), "NV")
    rec("y", [lambda: g.sync.dma_start(T.y[:], ap(Yw))], [Yw], [("y", 0, 1, 1)], kind="d")
    rec("g", [], [("y", 0, 1, 1)], [])

    hist = {}
    needed = set()
    for i, o in enumerate(ops):
        deps = set()
        both = [(x, False) for x in o["rd"]] + [(x, True) for x in o["wr"]]
        for x, w in both:
            psum = x[0] in SCRATCH and SCRATCH[x[0]][0] == "psum"
            for j, lo, hi, jw in hist.get(x[0], []):
                if (psum and ops[j]["q"] != o["q"]) or ((w or jw) and lo < x[2] and x[1] < hi):
                    deps.add(j)
        for x, w in both:
            hist.setdefault(x[0], []).append((i, x[1], x[2], w))
        o["deps"] = deps
    known = {}
    for i, o in enumerate(ops):
        k = known.get(o["q"], set())
        o["waits"] = []
        for j in sorted(o["deps"], reverse=True):
            if j not in k:
                assert ops[j]["kind"] != "r"
                o["waits"].append(j)
                needed.add(j)
                k = k | {j} | ops[j]["known"]
        o["known"] = k if o["q"] else set()
        if o["q"]:
            known[o["q"]] = k
    last, count, ndma = {}, {}, [0]
    queue = {"g": g, "v": g.vector, "s": g.scalar, "t": g.tensor, "y": g.sync}
    for i, o in enumerate(ops):
        if o["kind"] == "x":
            assert i in needed
            continue
        for j in o["waits"]:
            queue[o["q"]].wait_ge(T.sem[ops[j]["token"][0]], ops[j]["token"][1])
        name = None
        if o["kind"] == "d":
            assert i in needed
            name = "d%d" % ndma[0]
            ndma[0] += 1
            o["token"] = (name, 16)
        elif i in needed:
            free = [s for s in last if last[s] in o["known"]]
            name = free[0] if free else "c%d" % len(last)
            last[name] = i
            count[name] = count.get(name, 0) + (1 if o["acc"] else len(o["fns"]))
            o["token"] = (name, count[name])
        for n, fn in enumerate(o["fns"]):
            inst = fn()
            if name is not None and (not o["acc"] or n == len(o["fns"]) - 1):
                inst.then_inc(T.sem[name], 16 if o["kind"] == "d" else 1)
    g.wait_ge(T.sem.sent, sent[0])
